import numpy as np
CORES = [2,10,50,58,66,74,122]
N = 7
B, TIMES = 32, 2
def setup_inputs(rng):
    return {"x": (rng.standard_normal((N, 128, B), dtype=np.float32) * (0.5 + np.abs(rng.standard_normal((1, 1, B), dtype=np.float32))) / np.float32(np.sqrt(128 * N))), "a": (rng.standard_normal((N, 128, N * 128), dtype=np.float32) / 8)}
def setup_inputs_big(rng):
    d = setup_inputs(rng)
    for k in ("a",): d[k] = (d[k].astype(np.float32) * 1048576.0).astype(d[k].dtype)
    return d
def setup_inputs_small(rng):
    d = setup_inputs(rng)
    for k in ("a",): d[k] = (d[k].astype(np.float32) * (1 / 1048576.0)).astype(d[k].dtype)
    return d
def setup_inputs_apart(rng):
    d = setup_inputs(rng)
    f = (10.0 ** rng.permutation(np.linspace(-1.5, 1.5, N))).astype(np.float32).reshape(N, 1, 1)
    for k in ("a",): d[k] = (d[k].astype(np.float32) * f).astype(d[k].dtype)
    return d
def reference(x, a):
    X, A = x.astype(np.float64), a.astype(np.float64)
    h = X
    for _ in range(TIMES):
        h = np.stack([sum(A[r][:, 128 * j:128 * j + 128].T @ h[j] for j in range(N)) for r in range(N)])
        h = h / np.sqrt((h ** 2).sum(axis=(0, 1)))
        h = h + X
    return {"y": h.astype(np.float32)}

from concourse.bass import DstId, RemoteDMATransfer
from concourse.mybir import AluOpType, AxisListType, ActivationFunctionType

N = 7
B = 32
F32 = "float32"

SCRATCH = {
    "A": ("sbuf", [128, N * 128], F32),
    "H1": ("sbuf", [128, N * B], F32),
    "H2": ("sbuf", [128, N * B], F32),
    "SQ": ("sbuf", [128, N * B], F32),
    "SACC": ("sbuf", [128, B], F32),
    "ONES": ("sbuf", [128, 128], F32),
    "T1": ("sbuf", [128, B], F32),
    "II": ("sbuf", [128, B], F32),
    "M": ("sbuf", [128, 2 * B], F32),
    "MSG": ("sbuf", [128, 4], F32),
    "L": ("sbuf", [128, 8], F32),
    "JUNK": ("sbuf", [128, 8], F32),
    "ACC": ("sbuf", [128, 4], F32),
    "N1": ("sbuf", [128, B], F32),
    "S1D": ("sbuf", [128, B], F32),
    "D": ("sbuf", [128, B], F32),
    "DM": ("sbuf", [128, B], F32),
    "DCOL": ("sbuf", [128, 4], F32),
    "SC": ("sbuf", [128, 4], F32),
    "ROWN": ("sbuf", [128, B], F32),
    "R": ("sbuf", [128, B], F32),
    "V1": ("sbuf", [128, B], F32),
    "V": ("sbuf", [128, B], F32),
    "N2": ("sbuf", [128, B], F32),
    "R2": ("sbuf", [128, B], F32),
    "Y1": ("sbuf", [128, B], F32),
    "Y": ("sbuf", [128, B], F32),
    "U_PS": ("psum", [128, 512], F32),
    "W_PS": ("psum", [128, 512], F32),
    "S1_PS": ("psum", [128, 512], F32),
    "SS2_PS": ("psum", [128, 512], F32),
    "PQ_PS": ("psum", [128, 512], F32),
}

SEMAPHORES = (["x", "a", "ones", "msg0", "t1", "ii", "loc", "u", "ucopy", "w", "mq", "mp", "pq", "msg", "s1", "n1",
               "s1d", "d", "dm", "dcol", "sc", "rown", "v1", "v", "r3", "acc", "r", "ss2", "n2", "r2", "y1", "yr", "y"]
              + ["r1_%d" % j for j in range(N)] + ["r2_%d" % j for j in range(N)]
              + ["sq_%d" % j for j in range(N)] + ["ac_%d" % k for k in range(N)])


def rank_program(g, core, T, topo):
    me = T.rank_of(core)
    if me is None:
        return
    S = T.sem
    mult, add = AluOpType.mult, AluOpType.add
    Act = ActivationFunctionType
    te, ve, sc, sy = g.tensor, g.vector, g.scalar, g.sync

    outs = [(me + s) % N for s in range(1, N)]
    ins = [(me - s) % N for s in range(1, N)]

    def tile(buf, j):
        return buf[:, B * j:B * j + B]

    def atile(j):
        return T.A[:, 128 * j:128 * j + 128]

    mask = -1
    ids = []
    for q in outs:
        dst = T.cores[q]
        assert topo.may_write(core, dst)
        mask &= topo.mask(core, dst)
        rid, pid, _se = topo.addr(dst)
        ids.append(DstId(rid=rid, pnc=pid))
    neng = bin(mask).count("1")

    def send(src, dsts, sem):
        g.remote_dma_fused([RemoteDMATransfer(dst_ids=ids, dma_engine_mask=mask, remote_sem=sem,
                                              srcs=[src], dsts=dsts, alu_op=0)], local_sem=S.loc)

    sy.dma_start(tile(T.H1, me), T.x[:]).then_inc(S.x, 16)
    sy.dma_start(T.A[:], T.a[:]).then_inc(S.a, 16)

    g.wait_ge(S.x, 16)
    send(tile(T.H1, me), [tile(T.H1, me)] * len(outs), S["r1_%d" % me])
    g.wait_ge(S.ones, 1)
    g.affine_select(T.T1[0:64, :], T.ONES[0:64, 0:B], [[-1, B]], AluOpType.is_equal, 0.0, 0, 1).then_inc(S.t1, 1)
    g.wait_ge(S.t1, 1)
    g.affine_select(T.II[0:64, :], T.T1[0:64, :], [[-1, B]], AluOpType.not_equal, 1.0, -B, 1).then_inc(S.ii, 1)
    g.wait_ge(S.ucopy, 1)
    send(tile(T.H2, me), [tile(T.H2, me)] * len(outs), S["r2_%d" % me])
    g.wait_ge(S.msg, 1)
    send(T.MSG[:, 0:1], [T.L[:, s:s + 1] for s in range(N - 1)], S.r3)
    g.wait_ge(S.loc, 3 * neng)

    te.wait_ge(S.x, 16)
    te.wait_ge(S.a, 16)
    te.matmul(T.U_PS[:, 0:B], atile(me), tile(T.H1, me), True, False).then_inc(S.u, 1)
    for k, j in enumerate(ins):
        te.wait_ge(S["r1_%d" % j], neng)
        te.matmul(T.U_PS[:, 0:B], atile(j), tile(T.H1, j), False, k == N - 2).then_inc(S.u, 1)
    te.wait_ge(S.ucopy, 1)
    te.matmul(T.W_PS[:, 0:B], atile(me), tile(T.H2, me), True, False).then_inc(S.w, 1)
    for k, j in enumerate(ins):
        te.wait_ge(S["r2_%d" % j], neng)
        te.matmul(T.W_PS[:, 0:B], atile(j), tile(T.H2, j), False, k == N - 2).then_inc(S.w, 1)
    te.wait_ge(S.ones, 1)
    te.wait_ge(S.mp, 1)
    te.matmul(T.PQ_PS[0:64, 0:1], T.M[:, 0:2 * B], T.ONES[:, 0:1], True, True).then_inc(S.pq, 1)
    te.wait_ge(S["ac_%d" % (N - 1)], 1)
    te.matmul(T.S1_PS[:, 0:B], T.ONES[:], T.SACC[:], True, True).then_inc(S.s1, 1)
    te.wait_ge(S.s1d, 1)
    te.matmul(T.SS2_PS[:, 0:B], T.ONES[:], T.S1D[:], True, False).then_inc(S.ss2, 1)
    te.wait_ge(S.rown, 1)
    te.matmul(T.SS2_PS[:, 0:B], T.ONES[0:64, :], T.ROWN[0:64, :], False, False).then_inc(S.ss2, 1)
    te.wait_ge(S.r, 1)
    te.matmul(T.SS2_PS[:, 0:B], T.ONES[0:64, :], T.R[0:64, :], False, True).then_inc(S.ss2, 1)

    sc.wait_ge(S.ucopy, 1)
    sc.activation(tile(T.SQ, me), tile(T.H2, me), Act.Square).then_inc(S["sq_%d" % me], 1)
    for j in ins:
        sc.wait_ge(S["r2_%d" % j], neng)
        sc.activation(tile(T.SQ, j), tile(T.H2, j), Act.Square).then_inc(S["sq_%d" % j], 1)
    sc.wait_ge(S.mq, 1)
    sc.activation(T.M[:, 0:B], T.W_PS[:, 0:B], Act.Square).then_inc(S.mp, 1)
    sc.wait_ge(S.s1, 1)
    sc.activation(T.N1[:], T.S1_PS[:, 0:B], Act.Sqrt).then_inc(S.n1, 1)
    sc.activation(T.S1D[:], T.S1_PS[:, 0:B], Act.Copy, scale=1.0 / 128.0).then_inc(S.s1d, 1)
    sc.wait_ge(S.sc, 2)
    sc.wait_ge(S.r3, (N - 1) * neng)
    sc.activation(T.JUNK[0:64, 0:N - 1], T.L[0:64, 0:N - 1], Act.Identity, scale=T.SC[0:64, 0:1],
                  accum_out=T.ACC[0:64, 0:1]).then_inc(S.acc, 1)
    sc.wait_ge(S.ss2, 3)
    sc.activation(T.N2[:], T.SS2_PS[:, 0:B], Act.Sqrt).then_inc(S.n2, 1)

    ve.memset(T.ONES[:], 1.0).then_inc(S.ones, 1)
    ve.memset(T.MSG[:], 0.0).then_inc(S.msg0, 1)
    ve.wait_ge(S.u, N)
    ve.tensor_copy(tile(T.H2, me), T.U_PS[:, 0:B]).then_inc(S.ucopy, 1)
    ve.wait_ge(S["sq_%d" % me], 1)
    for k, j in enumerate(ins):
        ve.wait_ge(S["sq_%d" % j], 1)
        if k == 0:
            ve.tensor_tensor(T.SACC[:], tile(T.SQ, me), tile(T.SQ, j), add).then_inc(S["ac_%d" % (k + 1)], 1)
        else:
            ve.wait_ge(S["ac_%d" % k], 1)
            ve.tensor_tensor(T.SACC[:], T.SACC[:], tile(T.SQ, j), add).then_inc(S["ac_%d" % (k + 1)], 1)
    ve.wait_ge(S.w, N)
    ve.tensor_tensor(T.M[:, B:2 * B], T.W_PS[:, 0:B], tile(T.H2, me), mult).then_inc(S.mq, 1)
    ve.wait_ge(S.msg0, 1)
    ve.wait_ge(S.pq, 1)
    ve.tensor_copy(T.MSG[0:64, 0:1], T.PQ_PS[0:64, 0:1]).then_inc(S.msg, 1)
    ve.wait_ge(S.n1, 1)
    ve.reciprocal(T.D[:], T.N1[:]).then_inc(S.d, 1)
    ve.wait_ge(S.d, 1)
    ve.wait_ge(S.ii, 1)
    ve.tensor_tensor(T.DM[0:64, :], T.D[0:64, :], T.II[0:64, :], mult).then_inc(S.dm, 1)
    ve.wait_ge(S.dm, 1)
    ve.tensor_reduce(T.DCOL[0:64, 0:1], T.DM[0:64, :], AxisListType.X, add).then_inc(S.dcol, 1)
    ve.wait_ge(S.dcol, 1)
    ve.tensor_tensor(T.SC[0:32, 0:1], T.DCOL[0:32, 0:1], T.DCOL[0:32, 0:1], mult).then_inc(S.sc, 1)
    ve.tensor_scalar(T.SC[32:64, 0:1], T.DCOL[32:64, 0:1], 2.0, None, mult).then_inc(S.sc, 1)
    ve.wait_ge(S.sc, 2)
    ve.wait_ge(S.msg, 1)
    ve.tensor_scalar(T.ROWN[0:64, :], T.II[0:64, :], T.MSG[0:64, 0:1], T.SC[0:64, 0:1], mult, mult).then_inc(S.rown, 1)
    ve.wait_ge(S.mp, 1)
    ve.tensor_tensor(T.V1[:], T.W_PS[:, 0:B], T.D[:], mult).then_inc(S.v1, 1)
    ve.wait_ge(S.v1, 1)
    ve.tensor_tensor(T.V[:], T.V1[:], tile(T.H2, me), add).then_inc(S.v, 1)
    ve.wait_ge(S.acc, 1)
    ve.tensor_scalar(T.R[0:64, :], T.II[0:64, :], T.ACC[0:64, 0:1], None, mult).then_inc(S.r, 1)
    ve.wait_ge(S.n2, 1)
    ve.reciprocal(T.R2[:], T.N2[:]).then_inc(S.r2, 1)
    ve.wait_ge(S.r2, 1)
    ve.wait_ge(S.v, 1)
    ve.tensor_tensor(T.Y1[:], T.V[:], T.R2[:], mult).then_inc(S.y1, 1)
    ve.wait_ge(S.y1, 1)
    ve.wait_ge(S.x, 16)
    ve.tensor_tensor(T.Y[:], T.Y1[:], tile(T.H1, me), add).then_inc(S.yr, 1)

    sy.wait_ge(S.yr, 1)
    sy.dma_start(T.y[:], T.Y[:]).then_inc(S.y, 16)
    sy.wait_ge(S.y, 16)
